import numpy as np
import ml_dtypes


def mxq(x, axis, fmt="e4m3"):
    dtype, down = {"e4m3": (ml_dtypes.float8_e4m3fn, 7), "e5m2": (ml_dtypes.float8_e5m2, 14)}[fmt]
    v = np.moveaxis(np.asarray(x, np.float32).astype(ml_dtypes.bfloat16).astype(np.float64), axis, -1)
    blocks = v.reshape(v.shape[:-1] + (-1, 32))
    amax = np.abs(blocks).max(-1, keepdims=True)
    byte = np.maximum(np.where(amax > 0, np.frexp(amax)[1] - 1 + 127, 0) - down, 1)
    scale = np.exp2(byte - 127.0)
    codes = (blocks / scale).astype(np.float32).astype(dtype).astype(np.float64)
    return np.moveaxis((codes * scale).reshape(v.shape), -1, axis)


WIDE = False


def mx_kscale(k):
    if not WIDE:
        return np.ones(k)
    levels = np.array([30, -30])
    if k % 512:
        return np.exp2(np.random.permutation(np.resize(levels, k // 32))).repeat(32)
    a = np.empty((k // 512, 16))
    for p in range(k // 512):
        a[p, :8] = np.random.permutation(np.resize(levels, 8))
        for g in range(8):
            far = levels[np.abs(levels - a[p, g]) >= 10]
            a[p, g + 8] = far[np.random.randint(len(far))]
    return np.exp2(a.ravel()).repeat(32)


def f64(x):
    return np.asarray(x).astype(np.float64)


def striped(idx):
    return np.tile(np.asarray(idx).reshape(-1, 16).T, (8, 1)).astype(np.uint16)


def unstriped(offs):
    return offs[:16].T.reshape(-1).astype(np.int64)


E2M1 = np.array([0.0, 0.5, 1.0, 1.5, 2.0, 3.0, 4.0, 6.0, -0.0, -0.5, -1.0, -1.5, -2.0, -3.0, -4.0, -6.0])


def pack_weight(w, fmt):
    k, n = w.shape
    w = f64(np.asarray(w, np.float32).astype(ml_dtypes.bfloat16)).reshape(k // 32, 32, n)
    amax = np.abs(w).max(1)
    if fmt in ("e4m3", "e5m2"):
        byte = np.frexp(amax)[1] - 1 + 127 - (7 if fmt == "e4m3" else 14)
    else:
        mant, ex = np.frexp(amax / 6.0)
        byte = np.where(mant > 0.5, ex, ex - 1) + 127
    byte = np.clip(np.where(amax > 0, byte, 1), 1, 254)
    scaled = (w * np.exp2(127.0 - byte)[:, None, :]).reshape(k, n).astype(np.float32)
    by_word = np.ascontiguousarray(scaled.reshape(k // 512, 128, 4, n).transpose(0, 1, 3, 2))
    if fmt in ("e4m3", "e5m2"):
        words = by_word.astype(ml_dtypes.float8_e4m3fn if fmt == "e4m3" else ml_dtypes.float8_e5m2).view(np.uint8)
    else:
        c = by_word.astype(ml_dtypes.float4_e2m1fn).view(np.uint8) & 0xF
        words = (c[..., 0::2] | (c[..., 1::2] << 4)).reshape(k // 512, 128, 2 * n)
    return np.ascontiguousarray(words), np.ascontiguousarray(byte.astype(np.uint8).reshape(k // 512, 16, n))


def unpack_weight(words, scales, fmt):
    g, _, n = scales.shape
    words = np.ascontiguousarray(words).reshape(g, 128, n, -1)
    if fmt in ("e4m3", "e5m2"):
        vals = words.view(ml_dtypes.float8_e4m3fn if fmt == "e4m3" else ml_dtypes.float8_e5m2).astype(np.float64)
    else:
        nib = np.empty((g, 128, n, 4), np.uint8)
        nib[..., 0::2] = words & 0xF
        nib[..., 1::2] = words >> 4
        vals = E2M1[nib]
    vals = vals * np.repeat(np.exp2(scales.astype(np.float64) - 127.0), 8, axis=1)[..., None]
    return vals.transpose(0, 1, 3, 2).reshape(g * 512, n)


K, T, J, N = 1024, 1024, 256, 256


def setup_inputs():
    n = np.random.standard_normal
    idx = np.random.permutation(T)[:J]
    idx2 = np.random.permutation(T)[:J]
    fk = mx_kscale(K)
    xtp = pack_weight(n((K, T)) * np.random.uniform(0.4, 1.6, (1, T)) / fk[:, None], "e4m3")
    wap = pack_weight(n((K, N)) * 1 / np.sqrt(K) * fk[:, None], "e5m2")
    return {
        "xt_words": xtp[0],
        "xt_scales": xtp[1],
        "wa_words": wap[0],
        "wa_scales": wap[1],
        "wb": (n((K, N)) * 1 / np.sqrt(K) * fk[:, None]).astype(np.float32),
        "bi": (np.random.uniform(-0.6, 0.6, (1, N))).astype(np.float32),
        "gm": (np.random.uniform(0.5, 2.0, (1, N))).astype(np.float32),
        "offs": striped(idx),
        "offs2": striped(idx2),
    }


def reference(xt_words, xt_scales, wa_words, wa_scales, wb, bi, gm, offs, offs2):
    idx = unstriped(offs)
    idx2 = unstriped(offs2)
    xtu = unpack_weight(xt_words, xt_scales, "e4m3")
    wau = unpack_weight(wa_words, wa_scales, "e5m2")
    xtidxg = xtu[:, idx]
    a = xtidxg.T @ wau
    xtidx2g = xtu[:, idx2]
    wbq = mxq(f64(wb), 0, "e5m2")
    b0 = xtidx2g.T @ wbq
    b2 = b0 + f64(bi)
    d1 = np.mean(np.square(a - b2), axis=1, keepdims=True)
    y = a * f64(gm) / (0.4 + d1)
    return y

@@ -1,0 +1,163 @@
+import math
+from contextlib import ExitStack
+
+import concourse.mybir as mybir
+from concourse.masks import make_identity
+
+K, T, J, N = 1024, 1024, 256, 256
+FLOPS = 2 * 2 * J * K * N
+
+F32 = mybir.dt.float32
+BF16 = mybir.dt.bfloat16
+I32 = mybir.dt.int32
+U32 = mybir.dt.uint32
+U16 = mybir.dt.uint16
+U8 = mybir.dt.uint8
+E4M3X4 = mybir.dt.float8_e4m3fn_x4
+E5M2X4 = mybir.dt.float8_e5m2_x4
+ALU = mybir.AluOpType
+ACT = mybir.ActivationFunctionType
+
+P = 128
+PACK = 4
+PASSES = K // (P * PACK)
+QUADS = 4
+ROWS = 4
+TILES = J // P
+LISTS = 2
+EPS = 0.4
+SPLIT = 160
+
+
+def tile_list_rows_twotokens_bygapsize_kernel(
+    tc, xt_words, xt_scales, wa_words, wa_scales, wb, bi, gm, offs, offs2, out
+):
+    nc = tc.nc
+    with ExitStack() as ctx:
+        sb = ctx.enter_context(tc.tile_pool(name="sb", bufs=1))
+        ps = ctx.enter_context(tc.psum_pool(name="ps", bufs=1))
+
+        lists = [sb.tile([P, J // 16], U16, name=f"list{l}") for l in range(LISTS)]
+        xs_win = sb.tile([P, T], U8, align_bytes=64)
+        xw_win = [sb.tile([P, T], I32, name=f"xw_win{z}", align_bytes=64) for z in range(PASSES)]
+        wb_raw = [sb.tile([P, PACK, N], F32, name=f"wb_raw{z}", align_bytes=64) for z in range(PASSES)]
+        wa_codes = sb.tile([P, PASSES, N], I32, align_bytes=64)
+        staged = sb.tile([P, LISTS * J + N], U8, align_bytes=64)
+        planes = sb.tile([P, PASSES, LISTS * J + N], U8, align_bytes=64)
+        vec_cols = sb.tile([P, 4], F32)
+        ident = sb.tile([P, P], F32, align_bytes=64)
+        ones = sb.tile([P, 1], F32)
+        gap = [sb.tile([P, N + 1], F32, name=f"gap{t}", align_bytes=64) for t in range(TILES)]
+
+        nc.vector.memset(xs_win[32:64, :].bitcast(I32), 0)
+        nc.vector.memset(xs_win[64:128, :].bitcast(I32), 0)
+        nc.vector.memset(ones[:], 1.0)
+        nc.vector.memset(planes[:].rearrange("p z c -> p (z c)").bitcast(I32), 0)
+
+        nc.sync.dma_start(lists[0][:], offs)
+        nc.sync.dma_start(lists[1][:], offs2)
+        nc.scalar.dma_start(xs_win[0:32, :].bitcast(I32), xt_scales.rearrange("z q c -> q z c").bitcast(I32))
+        nc.scalar.dma_start(
+            staged[0:32, LISTS * J :].bitcast(I32), wa_scales.rearrange("z q c -> q z c").bitcast(I32)
+        )
+        nc.gpsimd.dma_start(vec_cols[0:64, :], bi.rearrange("o (p c) -> (o p) c", c=4))
+        nc.gpsimd.dma_start(vec_cols[64:128, :], gm.rearrange("o (p c) -> (o p) c", c=4))
+        make_identity(nc, ident[:])
+
+        def load_words(z):
+            nc.sync.dma_start(xw_win[z][:], xt_words[z].rearrange("p c r -> p (c r)").bitcast(I32))
+
+        def load_wb(z):
+            nc.sync.dma_start(wb_raw[z][:], wb[z * 512 : (z + 1) * 512, :].rearrange("(p j) n -> p j n", j=PACK))
+
+        load_words(0)
+        load_wb(0)
+        load_words(1)
+        nc.sync.dma_start(wa_codes[:], wa_words.rearrange("z p c r -> p z (c r)").bitcast(I32))
+        load_wb(1)
+        for t in range(TILES):
+            nc.scalar.activation(gap[t][:, N : N + 1], ones[:], ACT.Square, scale=(EPS * N) ** 0.25)
+
+        xs_got = sb.tile([P, LISTS, J], U8, align_bytes=64)
+        for l in range(LISTS):
+            nc.vector.tensor_copy(xs_got[:, l, :], xs_win[:].indirect(lists[l][:]))
+        nc.vector.tensor_copy(
+            staged[0:32, : LISTS * J].bitcast(I32), xs_got[0:32, :, :].rearrange("p l c -> p (l c)").bitcast(I32)
+        )
+        for q in range(QUADS):
+            nc.scalar.dma_start(
+                planes[32 * q : 32 * q + ROWS, :, :].bitcast(I32), staged[8 * q : 8 * q + 8, :].bitcast(I32)
+            )
+
+        rows_ps = ps.tile([P, 4, P], F32)
+        for c in range(4):
+            nc.tensor.transpose(rows_ps[:, c, :], vec_cols[:, c : c + 1].to_broadcast([P, P]), ident[:])
+        rows = sb.tile([P, 2, N], F32, align_bytes=64)
+        nc.scalar.copy(rows[:].rearrange("m v (p c) -> m (v p) c", c=4), rows_ps[:].rearrange("m c p -> m p c"))
+
+        x_got = [[sb.tile([P, J], U32, name=f"x_got{l}{z}", align_bytes=64) for z in range(PASSES)] for l in range(LISTS)]
+        wb_bf = [sb.tile([P, N, PACK], BF16, name=f"wb_bf{z}", align_bytes=64) for z in range(PASSES)]
+        wb_codes = [sb.tile([P, N], U32, name=f"wb_codes{z}", align_bytes=64) for z in range(PASSES)]
+        wb_plane = [sb.tile([P, N], U8, name=f"wb_plane{z}", align_bytes=64) for z in range(PASSES)]
+        acc = [[ps.tile([P, N], F32, name=f"acc{l}{t}") for t in range(TILES)] for l in range(LISTS)]
+
+        def product(l, z, t):
+            cols = slice(t * P, (t + 1) * P)
+            if l == 0:
+                rhs, rhs_scale = wa_codes[:, z, :], planes[:, z, LISTS * J :]
+            else:
+                rhs, rhs_scale = wb_codes[z][:], wb_plane[z][:]
+            nc.tensor.matmul_mx(
+                acc[l][t][:],
+                lhsT=x_got[l][z][:, cols].bitcast(E4M3X4),
+                lhsT_scale=planes[:, z, l * J + t * P : l * J + (t + 1) * P],
+                rhs=rhs.bitcast(E5M2X4),
+                rhs_scale=rhs_scale,
+                start=(z == 0),
+                stop=(z == PASSES - 1),
+            )
+
+        def cast(copy, z, cols):
+            copy(
+                wb_bf[z][:, cols, :].rearrange("p (c i) j -> p c j i", i=4),
+                wb_raw[z][:, :, cols].rearrange("p j (c i) -> p c j i", i=4),
+            )
+
+        def quantise(z):
+            nc.vector.quantize_mx(
+                out=wb_codes[z][:].bitcast(E5M2X4), scales=wb_plane[z][:], in_=wb_bf[z][:].rearrange("p n j -> p (n j)")
+            )
+
+        def gather_words(z):
+            for l in range(LISTS):
+                nc.vector.tensor_copy(x_got[l][z][:], xw_win[z][:].bitcast(U32).indirect(lists[l][:]))
+
+        gather_words(0)
+        cast(nc.scalar.copy, 0, slice(0, N))
+        quantise(0)
+        gather_words(1)
+        for t in range(TILES):
+            for z in range(PASSES):
+                product(0, z, t)
+        for t in range(TILES):
+            product(1, 0, t)
+        cast(nc.vector.tensor_copy, 1, slice(0, SPLIT))
+        cast(nc.scalar.copy, 1, slice(SPLIT, N))
+        quantise(1)
+        for t in range(TILES):
+            product(1, 1, t)
+
+        part = sb.tile([P, TILES, N], F32, tag="wb_bf1", align_bytes=64)
+        den = [sb.tile([P, 1], F32, name=f"den{t}") for t in range(TILES)]
+        inv = [sb.tile([P, 1], F32, name=f"inv{t}") for t in range(TILES)]
+        y = [sb.tile([P, N], F32, name=f"y{t}", align_bytes=64) for t in range(TILES)]
+        for t in range(TILES):
+            nc.vector.tensor_tensor(part[:, t, :], acc[0][t][:], rows[:, 0, :], ALU.subtract)
+        for t in range(TILES):
+            nc.vector.tensor_tensor(gap[t][:, :N], acc[1][t][:], part[:, t, :], ALU.subtract)
+            nc.scalar.activation(gap[t][:], gap[t][:], ACT.Square, scale=1.0 / math.sqrt(N), accum_out=den[t][:])
+        for t in range(TILES):
+            nc.vector.tensor_tensor(part[:, t, :], acc[0][t][:], rows[:, 1, :], ALU.mult)
+            nc.vector.reciprocal(inv[t][:], den[t][:])
+            nc.vector.tensor_scalar(y[t][:], part[:, t, :], inv[t][:], None, ALU.mult)
+            nc.sync.dma_start(out[t * P : (t + 1) * P, :], y[t][:])

@@ -44,7 +44,7 @@ def tile_list_rows_twotokens_bygapsize_kernel(
         wa_codes = sb.tile([P, PASSES, N], I32, align_bytes=64)
         staged = sb.tile([P, LISTS * J + N], U8, align_bytes=64)
         planes = sb.tile([P, PASSES, LISTS * J + N], U8, align_bytes=64)
-        vec_cols = sb.tile([P, 4], F32)
+        vec_cols = [sb.tile([P, 2], F32, name=f"vec_cols{v}") for v in range(2)]
         ident = sb.tile([P, P], F32, align_bytes=64)
         ones = sb.tile([P, 1], F32)
         gap = [sb.tile([P, N + 1], F32, name=f"gap{t}", align_bytes=64) for t in range(TILES)]
@@ -53,6 +53,7 @@ def tile_list_rows_twotokens_bygapsize_kernel(
         nc.vector.memset(xs_win[64:128, :].bitcast(I32), 0)
         nc.vector.memset(ones[:], 1.0)
         nc.vector.memset(planes[:].rearrange("p z c -> p (z c)").bitcast(I32), 0)
+        make_identity(nc, ident[:])
 
         nc.sync.dma_start(lists[0][:], offs)
         nc.sync.dma_start(lists[1][:], offs2)
@@ -60,9 +61,6 @@ def tile_list_rows_twotokens_bygapsize_kernel(
         nc.scalar.dma_start(
             staged[0:32, LISTS * J :].bitcast(I32), wa_scales.rearrange("z q c -> q z c").bitcast(I32)
         )
-        nc.gpsimd.dma_start(vec_cols[0:64, :], bi.rearrange("o (p c) -> (o p) c", c=4))
-        nc.gpsimd.dma_start(vec_cols[64:128, :], gm.rearrange("o (p c) -> (o p) c", c=4))
-        make_identity(nc, ident[:])
 
         def load_words(z):
             nc.sync.dma_start(xw_win[z][:], xt_words[z].rearrange("p c r -> p (c r)").bitcast(I32))
@@ -71,6 +69,8 @@ def tile_list_rows_twotokens_bygapsize_kernel(
             nc.sync.dma_start(wb_raw[z][:], wb[z * 512 : (z + 1) * 512, :].rearrange("(p j) n -> p j n", j=PACK))
 
         load_words(0)
+        for v, vec in enumerate((bi, gm)):
+            nc.sync.dma_start(vec_cols[v][:], vec.rearrange("o (p c) -> (o p) c", c=2))
         load_wb(0)
         load_words(1)
         nc.sync.dma_start(wa_codes[:], wa_words.rearrange("z p c r -> p z (c r)").bitcast(I32))
@@ -89,17 +89,18 @@ def tile_list_rows_twotokens_bygapsize_kernel(
                 planes[32 * q : 32 * q + ROWS, :, :].bitcast(I32), staged[8 * q : 8 * q + 8, :].bitcast(I32)
             )
 
-        rows_ps = ps.tile([P, 4, P], F32)
-        for c in range(4):
-            nc.tensor.transpose(rows_ps[:, c, :], vec_cols[:, c : c + 1].to_broadcast([P, P]), ident[:])
-        rows = sb.tile([P, 2, N], F32, align_bytes=64)
-        nc.scalar.copy(rows[:].rearrange("m v (p c) -> m (v p) c", c=4), rows_ps[:].rearrange("m c p -> m p c"))
+        rows = [sb.tile([P, N], F32, name=f"rows{v}", align_bytes=64) for v in range(2)]
+        for v in range(2):
+            spread = ps.tile([P, 2, P], F32, name=f"spread{v}", tag=f"bank{v}")
+            for c in range(2):
+                nc.tensor.transpose(spread[:, c, :], vec_cols[v][:, c : c + 1].to_broadcast([P, P]), ident[:])
+            nc.scalar.copy(rows[v][:].rearrange("m (p c) -> m p c", c=2), spread[:].rearrange("m c p -> m p c"))
 
         x_got = [[sb.tile([P, J], U32, name=f"x_got{l}{z}", align_bytes=64) for z in range(PASSES)] for l in range(LISTS)]
         wb_bf = [sb.tile([P, N, PACK], BF16, name=f"wb_bf{z}", align_bytes=64) for z in range(PASSES)]
         wb_codes = [sb.tile([P, N], U32, name=f"wb_codes{z}", align_bytes=64) for z in range(PASSES)]
         wb_plane = [sb.tile([P, N], U8, name=f"wb_plane{z}", align_bytes=64) for z in range(PASSES)]
-        acc = [[ps.tile([P, N], F32, name=f"acc{l}{t}") for t in range(TILES)] for l in range(LISTS)]
+        acc = [ps.tile([P, TILES, N], F32, name=f"acc{l}", tag=f"bank{l}") for l in range(LISTS)]
 
         def product(l, z, t):
             cols = slice(t * P, (t + 1) * P)
@@ -108,13 +109,13 @@ def tile_list_rows_twotokens_bygapsize_kernel(
             else:
                 rhs, rhs_scale = wb_codes[z][:], wb_plane[z][:]
             nc.tensor.matmul_mx(
-                acc[l][t][:],
+                acc[l][:, t, :],
                 lhsT=x_got[l][z][:, cols].bitcast(E4M3X4),
                 lhsT_scale=planes[:, z, l * J + t * P : l * J + (t + 1) * P],
                 rhs=rhs.bitcast(E5M2X4),
                 rhs_scale=rhs_scale,
-                start=(z == 0),
-                stop=(z == PASSES - 1),
+                start=(z == 0 and t == 0),
+                stop=(z == PASSES - 1 and t == TILES - 1),
             )
 
         def cast(copy, z, cols):
@@ -151,13 +152,13 @@ def tile_list_rows_twotokens_bygapsize_kernel(
         den = [sb.tile([P, 1], F32, name=f"den{t}") for t in range(TILES)]
         inv = [sb.tile([P, 1], F32, name=f"inv{t}") for t in range(TILES)]
         y = [sb.tile([P, N], F32, name=f"y{t}", align_bytes=64) for t in range(TILES)]
+        nc.vector.tensor_tensor(part[:], acc[0][:], rows[0][:].unsqueeze(1).to_broadcast([P, TILES, N]), ALU.subtract)
         for t in range(TILES):
-            nc.vector.tensor_tensor(part[:, t, :], acc[0][t][:], rows[:, 0, :], ALU.subtract)
-        for t in range(TILES):
-            nc.vector.tensor_tensor(gap[t][:, :N], acc[1][t][:], part[:, t, :], ALU.subtract)
+            nc.vector.tensor_tensor(gap[t][:, :N], acc[1][:, t, :], part[:, t, :], ALU.subtract)
             nc.scalar.activation(gap[t][:], gap[t][:], ACT.Square, scale=1.0 / math.sqrt(N), accum_out=den[t][:])
+        nc.vector.tensor_tensor(part[:], acc[0][:], rows[1][:].unsqueeze(1).to_broadcast([P, TILES, N]), ALU.mult)
         for t in range(TILES):
-            nc.vector.tensor_tensor(part[:, t, :], acc[0][t][:], rows[:, 1, :], ALU.mult)
             nc.vector.reciprocal(inv[t][:], den[t][:])
+        for t in range(TILES):
             nc.vector.tensor_scalar(y[t][:], part[:, t, :], inv[t][:], None, ALU.mult)
             nc.sync.dma_start(out[t * P : (t + 1) * P, :], y[t][:])

@@ -40,7 +40,7 @@ def tile_list_rows_twotokens_bygapsize_kernel(
         lists = [sb.tile([P, J // 16], U16, name=f"list{l}") for l in range(LISTS)]
         xs_win = sb.tile([P, T], U8, align_bytes=64)
         xw_win = [sb.tile([P, T], I32, name=f"xw_win{z}", align_bytes=64) for z in range(PASSES)]
-        wb_raw = [sb.tile([P, PACK, N], F32, name=f"wb_raw{z}", align_bytes=64) for z in range(PASSES)]
+        wb_raw = [sb.tile([P, PACK, N], F32, name="wb_raw0", align_bytes=64)]
         wa_codes = sb.tile([P, PASSES, N], I32, align_bytes=64)
         staged = sb.tile([P, LISTS * J + N], U8, align_bytes=64)
         planes = sb.tile([P, PASSES, LISTS * J + N], U8, align_bytes=64)
@@ -74,7 +74,6 @@ def tile_list_rows_twotokens_bygapsize_kernel(
         load_wb(0)
         load_words(1)
         nc.sync.dma_start(wa_codes[:], wa_words.rearrange("z p c r -> p z (c r)").bitcast(I32))
-        load_wb(1)
         for t in range(TILES):
             nc.scalar.activation(gap[t][:, N : N + 1], ones[:], ACT.Square, scale=(EPS * N) ** 0.25)
 
@@ -85,37 +84,43 @@ def tile_list_rows_twotokens_bygapsize_kernel(
             staged[0:32, : LISTS * J].bitcast(I32), xs_got[0:32, :, :].rearrange("p l c -> p (l c)").bitcast(I32)
         )
         for q in range(QUADS):
-            nc.scalar.dma_start(
+            nc.sync.dma_start(
                 planes[32 * q : 32 * q + ROWS, :, :].bitcast(I32), staged[8 * q : 8 * q + 8, :].bitcast(I32)
             )
+        wb_raw.append(sb.tile([P, PACK, N], F32, name="wb_raw1", tag="xs_got", align_bytes=64))
+        load_wb(1)
 
         rows = [sb.tile([P, N], F32, name=f"rows{v}", align_bytes=64) for v in range(2)]
-        for v in range(2):
-            spread = ps.tile([P, 2, P], F32, name=f"spread{v}", tag=f"bank{v}")
-            for c in range(2):
-                nc.tensor.transpose(spread[:, c, :], vec_cols[v][:, c : c + 1].to_broadcast([P, P]), ident[:])
-            nc.scalar.copy(rows[v][:].rearrange("m (p c) -> m p c", c=2), spread[:].rearrange("m c p -> m p c"))
+        spread = ps.tile([P, 2, P], F32, tag="bank_a")
+        for c in range(2):
+            nc.tensor.transpose(spread[:, c, :], vec_cols[0][:, c : c + 1].to_broadcast([P, P]), ident[:])
+        nc.scalar.copy(rows[0][:].rearrange("m (p c) -> m p c", c=2), spread[:].rearrange("m c p -> m p c"))
+        for c in range(2):
+            half = ps.tile([P, P], F32, name=f"half{c}", tag=f"bank_b{c}")
+            nc.tensor.transpose(half[:], vec_cols[1][:, c : c + 1].to_broadcast([P, P]), ident[:])
+            nc.scalar.copy(rows[1][:].rearrange("m (p c) -> m p c", c=2)[:, :, c], half[:])
 
         x_got = [[sb.tile([P, J], U32, name=f"x_got{l}{z}", align_bytes=64) for z in range(PASSES)] for l in range(LISTS)]
         wb_bf = [sb.tile([P, N, PACK], BF16, name=f"wb_bf{z}", align_bytes=64) for z in range(PASSES)]
         wb_codes = [sb.tile([P, N], U32, name=f"wb_codes{z}", align_bytes=64) for z in range(PASSES)]
         wb_plane = [sb.tile([P, N], U8, name=f"wb_plane{z}", align_bytes=64) for z in range(PASSES)]
-        acc = [ps.tile([P, TILES, N], F32, name=f"acc{l}", tag=f"bank{l}") for l in range(LISTS)]
+        acc_a = ps.tile([P, TILES, N], F32, tag="bank_a")
+        acc_b = [ps.tile([P, N], F32, name=f"acc_b{t}", tag=f"bank_b{t}") for t in range(TILES)]
 
         def product(l, z, t):
             cols = slice(t * P, (t + 1) * P)
             if l == 0:
-                rhs, rhs_scale = wa_codes[:, z, :], planes[:, z, LISTS * J :]
+                acc, rhs, rhs_scale = acc_a[:, t, :], wa_codes[:, z, :], planes[:, z, LISTS * J :]
             else:
-                rhs, rhs_scale = wb_codes[z][:], wb_plane[z][:]
+                acc, rhs, rhs_scale = acc_b[t][:], wb_codes[z][:], wb_plane[z][:]
             nc.tensor.matmul_mx(
-                acc[l][:, t, :],
+                acc,
                 lhsT=x_got[l][z][:, cols].bitcast(E4M3X4),
                 lhsT_scale=planes[:, z, l * J + t * P : l * J + (t + 1) * P],
                 rhs=rhs.bitcast(E5M2X4),
                 rhs_scale=rhs_scale,
-                start=(z == 0 and t == 0),
-                stop=(z == PASSES - 1 and t == TILES - 1),
+                start=(z == 0),
+                stop=(z == PASSES - 1),
             )
 
         def cast(copy, z, cols):
@@ -151,14 +156,14 @@ def tile_list_rows_twotokens_bygapsize_kernel(
         part = sb.tile([P, TILES, N], F32, tag="wb_bf1", align_bytes=64)
         den = [sb.tile([P, 1], F32, name=f"den{t}") for t in range(TILES)]
         inv = [sb.tile([P, 1], F32, name=f"inv{t}") for t in range(TILES)]
-        y = [sb.tile([P, N], F32, name=f"y{t}", align_bytes=64) for t in range(TILES)]
-        nc.vector.tensor_tensor(part[:], acc[0][:], rows[0][:].unsqueeze(1).to_broadcast([P, TILES, N]), ALU.subtract)
+        nc.vector.tensor_tensor(part[:], acc_a[:], rows[0][:].unsqueeze(1).to_broadcast([P, TILES, N]), ALU.subtract)
         for t in range(TILES):
-            nc.vector.tensor_tensor(gap[t][:, :N], acc[1][:, t, :], part[:, t, :], ALU.subtract)
+            nc.vector.tensor_tensor(gap[t][:, :N], acc_b[t][:], part[:, t, :], ALU.subtract)
             nc.scalar.activation(gap[t][:], gap[t][:], ACT.Square, scale=1.0 / math.sqrt(N), accum_out=den[t][:])
-        nc.vector.tensor_tensor(part[:], acc[0][:], rows[1][:].unsqueeze(1).to_broadcast([P, TILES, N]), ALU.mult)
+        nc.vector.tensor_tensor(part[:, 1, :], acc_a[:, 1, :], rows[1][:], ALU.mult)
         for t in range(TILES):
             nc.vector.reciprocal(inv[t][:], den[t][:])
-        for t in range(TILES):
-            nc.vector.tensor_scalar(y[t][:], part[:, t, :], inv[t][:], None, ALU.mult)
-            nc.sync.dma_start(out[t * P : (t + 1) * P, :], y[t][:])
+        nc.vector.scalar_tensor_tensor(gap[1][:, :N], acc_a[:, 0, :], inv[0][:], rows[1][:], ALU.mult, ALU.mult)
+        nc.sync.dma_start(out[0:P, :], gap[1][:, :N])
+        nc.vector.tensor_scalar(gap[0][:, :N], part[:, 1, :], inv[1][:], None, ALU.mult)
+        nc.sync.dma_start(out[P : 2 * P, :], gap[0][:, :N])

@@ -26,7 +26,7 @@ ROWS = 4
 TILES = J // P
 LISTS = 2
 EPS = 0.4
-SPLIT = 160
+SPLIT = 176
 
 
 def tile_list_rows_twotokens_bygapsize_kernel(
@@ -107,20 +107,20 @@ def tile_list_rows_twotokens_bygapsize_kernel(
         acc_a = ps.tile([P, TILES, N], F32, tag="bank_a")
         acc_b = [ps.tile([P, N], F32, name=f"acc_b{t}", tag=f"bank_b{t}") for t in range(TILES)]
 
-        def product(l, z, t):
+        def product(l, z, t, outs):
             cols = slice(t * P, (t + 1) * P)
             if l == 0:
                 acc, rhs, rhs_scale = acc_a[:, t, :], wa_codes[:, z, :], planes[:, z, LISTS * J :]
             else:
                 acc, rhs, rhs_scale = acc_b[t][:], wb_codes[z][:], wb_plane[z][:]
             nc.tensor.matmul_mx(
-                acc,
+                acc[:, outs],
                 lhsT=x_got[l][z][:, cols].bitcast(E4M3X4),
                 lhsT_scale=planes[:, z, l * J + t * P : l * J + (t + 1) * P],
-                rhs=rhs.bitcast(E5M2X4),
-                rhs_scale=rhs_scale,
+                rhs=rhs[:, outs].bitcast(E5M2X4),
+                rhs_scale=rhs_scale[:, outs],
                 start=(z == 0),
-                stop=(z == PASSES - 1),
+                stop=(z == PASSES - 1 and outs.stop == N),
             )
 
         def cast(copy, z, cols):
@@ -129,9 +129,11 @@ def tile_list_rows_twotokens_bygapsize_kernel(
                 wb_raw[z][:, :, cols].rearrange("p j (c i) -> p c j i", i=4),
             )
 
-        def quantise(z):
+        def quantise(z, outs):
             nc.vector.quantize_mx(
-                out=wb_codes[z][:].bitcast(E5M2X4), scales=wb_plane[z][:], in_=wb_bf[z][:].rearrange("p n j -> p (n j)")
+                out=wb_codes[z][:, outs].bitcast(E5M2X4),
+                scales=wb_plane[z][:, outs],
+                in_=wb_bf[z][:, outs, :].rearrange("p n j -> p (n j)"),
             )
 
         def gather_words(z):
@@ -140,23 +142,27 @@ def tile_list_rows_twotokens_bygapsize_kernel(
 
         gather_words(0)
         cast(nc.scalar.copy, 0, slice(0, N))
-        quantise(0)
+        quantise(0, slice(0, N))
         gather_words(1)
         for t in range(TILES):
             for z in range(PASSES):
-                product(0, z, t)
+                product(0, z, t, slice(0, N))
         for t in range(TILES):
-            product(1, 0, t)
-        cast(nc.vector.tensor_copy, 1, slice(0, SPLIT))
+            product(1, 0, t, slice(0, N))
+        halves = (slice(0, N // 2), slice(N // 2, N))
+        cast(nc.vector.tensor_copy, 1, halves[0])
+        cast(nc.vector.tensor_copy, 1, slice(N // 2, SPLIT))
         cast(nc.scalar.copy, 1, slice(SPLIT, N))
-        quantise(1)
-        for t in range(TILES):
-            product(1, 1, t)
+        for outs in halves:
+            quantise(1, outs)
+            for t in range(TILES):
+                product(1, 1, t, outs)
 
-        part = sb.tile([P, TILES, N], F32, tag="wb_bf1", align_bytes=64)
+        part = sb.tile([P, TILES, N], F32, tag="xs_got", align_bytes=64)
         den = [sb.tile([P, 1], F32, name=f"den{t}") for t in range(TILES)]
         inv = [sb.tile([P, 1], F32, name=f"inv{t}") for t in range(TILES)]
-        nc.vector.tensor_tensor(part[:], acc_a[:], rows[0][:].unsqueeze(1).to_broadcast([P, TILES, N]), ALU.subtract)
+        for t in range(TILES):
+            nc.vector.tensor_tensor(part[:, t, :], acc_a[:, t, :], rows[0][:], ALU.subtract)
         for t in range(TILES):
             nc.vector.tensor_tensor(gap[t][:, :N], acc_b[t][:], part[:, t, :], ALU.subtract)
             nc.scalar.activation(gap[t][:], gap[t][:], ACT.Square, scale=1.0 / math.sqrt(N), accum_out=den[t][:])

import math
from contextlib import ExitStack

import concourse.mybir as mybir
from concourse.masks import make_identity

K, T, J, N = 1024, 1024, 256, 256
FLOPS = 2 * 2 * J * K * N

F32 = mybir.dt.float32
BF16 = mybir.dt.bfloat16
I32 = mybir.dt.int32
U32 = mybir.dt.uint32
U16 = mybir.dt.uint16
U8 = mybir.dt.uint8
E4M3X4 = mybir.dt.float8_e4m3fn_x4
E5M2X4 = mybir.dt.float8_e5m2_x4
ALU = mybir.AluOpType
ACT = mybir.ActivationFunctionType

P = 128
PACK = 4
PASSES = K // (P * PACK)
QUADS = 4
ROWS = 4
TILES = J // P
LISTS = 2
EPS = 0.4
SPLIT = 176


def tile_list_rows_twotokens_bygapsize_kernel(
    tc, xt_words, xt_scales, wa_words, wa_scales, wb, bi, gm, offs, offs2, out
):
    nc = tc.nc
    with ExitStack() as ctx:
        sb = ctx.enter_context(tc.tile_pool(name="sb", bufs=1))
        ps = ctx.enter_context(tc.psum_pool(name="ps", bufs=1))

        lists = [sb.tile([P, J // 16], U16, name=f"list{l}") for l in range(LISTS)]
        xs_win = sb.tile([P, T], U8, align_bytes=64)
        xw_win = [sb.tile([P, T], I32, name=f"xw_win{z}", align_bytes=64) for z in range(PASSES)]
        wb_raw = [sb.tile([P, PACK, N], F32, name="wb_raw0", align_bytes=64)]
        wa_codes = sb.tile([P, PASSES, N], I32, align_bytes=64)
        staged = sb.tile([P, LISTS * J + N], U8, align_bytes=64)
        planes = sb.tile([P, PASSES, LISTS * J + N], U8, align_bytes=64)
        vec_cols = [sb.tile([P, 2], F32, name=f"vec_cols{v}") for v in range(2)]
        ident = sb.tile([P, P], F32, align_bytes=64)
        ones = sb.tile([P, 1], F32)
        gap = [sb.tile([P, N + 1], F32, name=f"gap{t}", align_bytes=64) for t in range(TILES)]

        nc.vector.memset(xs_win[32:64, :].bitcast(I32), 0)
        nc.vector.memset(xs_win[64:128, :].bitcast(I32), 0)
        nc.vector.memset(ones[:], 1.0)
        nc.vector.memset(planes[:].rearrange("p z c -> p (z c)").bitcast(I32), 0)
        make_identity(nc, ident[:])

        nc.sync.dma_start(lists[0][:], offs)
        nc.sync.dma_start(lists[1][:], offs2)
        nc.scalar.dma_start(xs_win[0:32, :].bitcast(I32), xt_scales.rearrange("z q c -> q z c").bitcast(I32))
        nc.scalar.dma_start(
            staged[0:32, LISTS * J :].bitcast(I32), wa_scales.rearrange("z q c -> q z c").bitcast(I32)
        )

        def load_words(z):
            nc.sync.dma_start(xw_win[z][:], xt_words[z].rearrange("p c r -> p (c r)").bitcast(I32))

        def load_wb(z):
            nc.sync.dma_start(wb_raw[z][:], wb[z * 512 : (z + 1) * 512, :].rearrange("(p j) n -> p j n", j=PACK))

        load_words(0)
        for v, vec in enumerate((bi, gm)):
            nc.sync.dma_start(vec_cols[v][:], vec.rearrange("o (p c) -> (o p) c", c=2))
        load_wb(0)
        load_words(1)
        nc.sync.dma_start(wa_codes[:], wa_words.rearrange("z p c r -> p z (c r)").bitcast(I32))
        for t in range(TILES):
            nc.scalar.activation(gap[t][:, N : N + 1], ones[:], ACT.Square, scale=(EPS * N) ** 0.25)

        xs_got = sb.tile([P, LISTS, J], U8, align_bytes=64)
        for l in range(LISTS):
            nc.vector.tensor_copy(xs_got[:, l, :], xs_win[:].indirect(lists[l][:]))
        nc.vector.tensor_copy(
            staged[0:32, : LISTS * J].bitcast(I32), xs_got[0:32, :, :].rearrange("p l c -> p (l c)").bitcast(I32)
        )
        for q in range(QUADS):
            nc.sync.dma_start(
                planes[32 * q : 32 * q + ROWS, :, :].bitcast(I32), staged[8 * q : 8 * q + 8, :].bitcast(I32)
            )
        wb_raw.append(sb.tile([P, PACK, N], F32, name="wb_raw1", tag="xs_got", align_bytes=64))
        load_wb(1)

        rows = [sb.tile([P, N], F32, name=f"rows{v}", align_bytes=64) for v in range(2)]
        spread = ps.tile([P, 2, P], F32, tag="bank_a")
        for c in range(2):
            nc.tensor.transpose(spread[:, c, :], vec_cols[0][:, c : c + 1].to_broadcast([P, P]), ident[:])
        nc.scalar.copy(rows[0][:].rearrange("m (p c) -> m p c", c=2), spread[:].rearrange("m c p -> m p c"))
        for c in range(2):
            half = ps.tile([P, P], F32, name=f"half{c}", tag=f"bank_b{c}")
            nc.tensor.transpose(half[:], vec_cols[1][:, c : c + 1].to_broadcast([P, P]), ident[:])
            nc.scalar.copy(rows[1][:].rearrange("m (p c) -> m p c", c=2)[:, :, c], half[:])

        x_got = [[sb.tile([P, J], U32, name=f"x_got{l}{z}", align_bytes=64) for z in range(PASSES)] for l in range(LISTS)]
        wb_bf = [sb.tile([P, N, PACK], BF16, name=f"wb_bf{z}", align_bytes=64) for z in range(PASSES)]
        wb_codes = [sb.tile([P, N], U32, name=f"wb_codes{z}", align_bytes=64) for z in range(PASSES)]
        wb_plane = [sb.tile([P, N], U8, name=f"wb_plane{z}", align_bytes=64) for z in range(PASSES)]
        acc_a = ps.tile([P, TILES, N], F32, tag="bank_a")
        acc_b = [ps.tile([P, N], F32, name=f"acc_b{t}", tag=f"bank_b{t}") for t in range(TILES)]

        def product(l, z, t, outs):
            cols = slice(t * P, (t + 1) * P)
            if l == 0:
                acc, rhs, rhs_scale = acc_a[:, t, :], wa_codes[:, z, :], planes[:, z, LISTS * J :]
            else:
                acc, rhs, rhs_scale = acc_b[t][:], wb_codes[z][:], wb_plane[z][:]
            nc.tensor.matmul_mx(
                acc[:, outs],
                lhsT=x_got[l][z][:, cols].bitcast(E4M3X4),
                lhsT_scale=planes[:, z, l * J + t * P : l * J + (t + 1) * P],
                rhs=rhs[:, outs].bitcast(E5M2X4),
                rhs_scale=rhs_scale[:, outs],
                start=(z == 0),
                stop=(z == PASSES - 1 and outs.stop == N),
            )

        def cast(copy, z, cols):
            copy(
                wb_bf[z][:, cols, :].rearrange("p (c i) j -> p c j i", i=4),
                wb_raw[z][:, :, cols].rearrange("p j (c i) -> p c j i", i=4),
            )

        def quantise(z, outs):
            nc.vector.quantize_mx(
                out=wb_codes[z][:, outs].bitcast(E5M2X4),
                scales=wb_plane[z][:, outs],
                in_=wb_bf[z][:, outs, :].rearrange("p n j -> p (n j)"),
            )

        def gather_words(z):
            for l in range(LISTS):
                nc.vector.tensor_copy(x_got[l][z][:], xw_win[z][:].bitcast(U32).indirect(lists[l][:]))

        gather_words(0)
        cast(nc.scalar.copy, 0, slice(0, N))
        quantise(0, slice(0, N))
        gather_words(1)
        for t in range(TILES):
            for z in range(PASSES):
                product(0, z, t, slice(0, N))
        for t in range(TILES):
            product(1, 0, t, slice(0, N))
        halves = (slice(0, N // 2), slice(N // 2, N))
        cast(nc.vector.tensor_copy, 1, halves[0])
        cast(nc.vector.tensor_copy, 1, slice(N // 2, SPLIT))
        cast(nc.scalar.copy, 1, slice(SPLIT, N))
        for outs in halves:
            quantise(1, outs)
            for t in range(TILES):
                product(1, 1, t, outs)

        part = sb.tile([P, TILES, N], F32, tag="xs_got", align_bytes=64)
        den = [sb.tile([P, 1], F32, name=f"den{t}") for t in range(TILES)]
        inv = [sb.tile([P, 1], F32, name=f"inv{t}") for t in range(TILES)]
        for t in range(TILES):
            nc.vector.tensor_tensor(part[:, t, :], acc_a[:, t, :], rows[0][:], ALU.subtract)
        for t in range(TILES):
            nc.vector.tensor_tensor(gap[t][:, :N], acc_b[t][:], part[:, t, :], ALU.subtract)
            nc.scalar.activation(gap[t][:], gap[t][:], ACT.Square, scale=1.0 / math.sqrt(N), accum_out=den[t][:])
        nc.vector.tensor_tensor(part[:, 1, :], acc_a[:, 1, :], rows[1][:], ALU.mult)
        for t in range(TILES):
            nc.vector.reciprocal(inv[t][:], den[t][:])
        nc.vector.scalar_tensor_tensor(gap[1][:, :N], acc_a[:, 0, :], inv[0][:], rows[1][:], ALU.mult, ALU.mult)
        nc.sync.dma_start(out[0:P, :], gap[1][:, :N])
        nc.vector.tensor_scalar(gap[0][:, :N], part[:, 1, :], inv[1][:], None, ALU.mult)
        nc.sync.dma_start(out[P : 2 * P, :], gap[0][:, :N])
